import numpy as np
import ml_dtypes

BF16 = ml_dtypes.bfloat16


def bf(x):
    return np.asarray(x, np.float32).astype(BF16)


def f32(x):
    return np.asarray(x, np.float32)


def f64(x):
    return np.asarray(x).astype(np.float64)


def striped(idx):
    return np.tile(idx.reshape(-1, 16).T, (8, 1))


S, K, M, N, E, Q = 512, 128, 128, 512, 8, 64


def setup_inputs():
    return {"table": bf(np.random.standard_normal((S, K))), "w": bf(np.random.standard_normal((E, K, M)) / np.sqrt(K)), "c": f32(0.2 + 0.8 * np.random.random_sample((1, N))), "offs": striped(np.sort(np.random.permutation(S).reshape(E, Q), axis=1).reshape(-1))}


def reference(table, w, c, offs):
    idx = offs[:16].T.reshape(-1)
    x = f64(table)[idx].T
    y = np.concatenate([f64(w)[e].T @ x[:, e * Q : (e + 1) * Q] for e in range(E)], axis=1)
    return y * f64(c)

@@ -1,0 +1,102 @@
+import concourse.mybir as mybir
+from concourse.masks import make_identity
+
+BF16, F32, U16 = mybir.dt.bfloat16, mybir.dt.float32, mybir.dt.uint16
+
+P = 128
+S = 512
+K = 128
+M = 128
+N = 512
+E = 8
+Q = N // E
+LIST_COLUMNS = Q // 16
+HALVES = 2
+PIECES = 4
+BLOCKS = S // P
+STRIDE = N // P
+WARM_UPS = 16
+
+FLOPS = 2 * K * M * N
+
+
+def tile_gather_matmul_kernel(tc, table, w, c, offs, out):
+    nc = tc.nc
+    with (
+        tc.tile_pool(name="held", bufs=1) as held,
+        tc.psum_pool(name="psum", bufs=1) as psum,
+    ):
+        offsets = held.tile([P, N // 16], U16, name="offsets")
+        nc.sync.dma_start(offsets[:], offs)
+        gain_columns = held.tile([P, STRIDE], F32, name="gain_columns")
+        nc.sync.dma_start(gain_columns[:], c.rearrange("o (p r) -> p (o r)", r=STRIDE))
+        rows = []
+        for h in range(HALVES):
+            rows_half = held.tile([P, BLOCKS // HALVES, K], BF16, name=f"rows{h}")
+            tokens_of_half = table[h * (S // HALVES) : (h + 1) * (S // HALVES)]
+            nc.scalar.dma_start(rows_half[:], tokens_of_half.rearrange("(b p) k -> p b k", p=P))
+            rows.append(rows_half)
+        weights = []
+        for h in range(HALVES):
+            weights_half = held.tile([K, E // HALVES, M], BF16, name=f"weights{h}")
+            experts = w[h * (E // HALVES) : (h + 1) * (E // HALVES)]
+            nc.scalar.dma_start(weights_half[:], experts.rearrange("e k m -> k e m"))
+            weights.append(weights_half)
+
+        zeros = held.tile([P, P], BF16, name="zeros")
+        nc.gpsimd.memset(zeros[:], 0.0)
+        unread = psum.tile([P, P], F32, name="unread")
+        for i in range(WARM_UPS):
+            nc.tensor.matmul(unread[:], zeros[:], zeros[:], start=True, stop=True)
+
+        identity = held.tile([P, P], BF16, name="identity")
+        make_identity(nc, identity[:])
+        tokens = held.tile([K, S], BF16, name="tokens")
+        for h in range(HALVES):
+            flipped = psum.tile([K, S // HALVES], BF16, name=f"flipped{h}")
+            for b in range(BLOCKS // HALVES):
+                nc.tensor.transpose(flipped[:, b * P : (b + 1) * P], rows[h][:, b, :], identity[:])
+            half = tokens[:, h * (S // HALVES) : (h + 1) * (S // HALVES)]
+            if h == 0:
+                nc.scalar.copy(half, flipped[:])
+            else:
+                nc.vector.tensor_copy(half, flipped[:])
+
+        identity32 = held.tile([P, P], F32, name="identity32")
+        nc.vector.tensor_copy(identity32[:], identity[:])
+        spread = psum.tile([M, N], F32, name="spread")
+        for r in range(STRIDE):
+            nc.tensor.transpose(
+                spread[:, r * P : (r + 1) * P],
+                gain_columns[:, r : r + 1].to_broadcast([P, M]),
+                identity32[:],
+            )
+        in_list_order = spread[:].rearrange("m (r p) -> m p r", r=STRIDE)
+        gains = held.tile([M, N], F32, name="gains")
+        for h in range(HALVES):
+            nc.scalar.copy(
+                gains[:, h * (N // HALVES) : (h + 1) * (N // HALVES)].rearrange(
+                    "m (p r) -> m p r", r=STRIDE
+                ),
+                in_list_order[:, h * (P // HALVES) : (h + 1) * (P // HALVES), :],
+            )
+
+        scaled = held.tile([M, N], F32, name="scaled")
+        for g in range(PIECES):
+            columns = slice(g * (N // PIECES), (g + 1) * (N // PIECES))
+            product = psum.tile([M, N // PIECES], F32, name=f"product{g}")
+            for i in range(E // PIECES):
+                e = g * (E // PIECES) + i
+                picked = tokens[:].indirect(offsets[:, e * LIST_COLUMNS : (e + 1) * LIST_COLUMNS])
+                nc.tensor.matmul(
+                    product[:, i * Q : (i + 1) * Q],
+                    weights[e // (E // HALVES)][:, e % (E // HALVES), :],
+                    picked,
+                    start=True,
+                    stop=True,
+                )
+            nc.vector.tensor_tensor(
+                scaled[:, columns], product[:], gains[:, columns], mybir.AluOpType.mult
+            )
+            queue = nc.sync if g % 2 == 0 else nc.scalar
+            queue.dma_start(out[:, columns], scaled[:, columns])

@@ -15,7 +15,7 @@ HALVES = 2
 PIECES = 4
 BLOCKS = S // P
 STRIDE = N // P
-WARM_UPS = 16
+WARM_UPS = 12
 
 FLOPS = 2 * K * M * N
 
@@ -26,10 +26,10 @@ def tile_gather_matmul_kernel(tc, table, w, c, offs, out):
         tc.tile_pool(name="held", bufs=1) as held,
         tc.psum_pool(name="psum", bufs=1) as psum,
     ):
-        offsets = held.tile([P, N // 16], U16, name="offsets")
-        nc.sync.dma_start(offsets[:], offs)
         gain_columns = held.tile([P, STRIDE], F32, name="gain_columns")
         nc.sync.dma_start(gain_columns[:], c.rearrange("o (p r) -> p (o r)", r=STRIDE))
+        offsets = held.tile([P, N // 16], U16, name="offsets")
+        nc.sync.dma_start(offsets[:], offs)
         rows = []
         for h in range(HALVES):
             rows_half = held.tile([P, BLOCKS // HALVES, K], BF16, name=f"rows{h}")
@@ -51,17 +51,6 @@ def tile_gather_matmul_kernel(tc, table, w, c, offs, out):
 
         identity = held.tile([P, P], BF16, name="identity")
         make_identity(nc, identity[:])
-        tokens = held.tile([K, S], BF16, name="tokens")
-        for h in range(HALVES):
-            flipped = psum.tile([K, S // HALVES], BF16, name=f"flipped{h}")
-            for b in range(BLOCKS // HALVES):
-                nc.tensor.transpose(flipped[:, b * P : (b + 1) * P], rows[h][:, b, :], identity[:])
-            half = tokens[:, h * (S // HALVES) : (h + 1) * (S // HALVES)]
-            if h == 0:
-                nc.scalar.copy(half, flipped[:])
-            else:
-                nc.vector.tensor_copy(half, flipped[:])
-
         identity32 = held.tile([P, P], F32, name="identity32")
         nc.vector.tensor_copy(identity32[:], identity[:])
         spread = psum.tile([M, N], F32, name="spread")
@@ -80,6 +69,13 @@ def tile_gather_matmul_kernel(tc, table, w, c, offs, out):
                 ),
                 in_list_order[:, h * (P // HALVES) : (h + 1) * (P // HALVES), :],
             )
+
+        tokens = held.tile([K, S], BF16, name="tokens")
+        for h in range(HALVES):
+            flipped = psum.tile([K, S // HALVES], BF16, name=f"flipped{h}")
+            for b in range(BLOCKS // HALVES):
+                nc.tensor.transpose(flipped[:, b * P : (b + 1) * P], rows[h][:, b, :], identity[:])
+            nc.vector.tensor_copy(tokens[:, h * (S // HALVES) : (h + 1) * (S // HALVES)], flipped[:])
 
         scaled = held.tile([M, N], F32, name="scaled")
         for g in range(PIECES):

@@ -30,18 +30,10 @@ def tile_gather_matmul_kernel(tc, table, w, c, offs, out):
         nc.sync.dma_start(gain_columns[:], c.rearrange("o (p r) -> p (o r)", r=STRIDE))
         offsets = held.tile([P, N // 16], U16, name="offsets")
         nc.sync.dma_start(offsets[:], offs)
-        rows = []
-        for h in range(HALVES):
-            rows_half = held.tile([P, BLOCKS // HALVES, K], BF16, name=f"rows{h}")
-            tokens_of_half = table[h * (S // HALVES) : (h + 1) * (S // HALVES)]
-            nc.scalar.dma_start(rows_half[:], tokens_of_half.rearrange("(b p) k -> p b k", p=P))
-            rows.append(rows_half)
-        weights = []
-        for h in range(HALVES):
-            weights_half = held.tile([K, E // HALVES, M], BF16, name=f"weights{h}")
-            experts = w[h * (E // HALVES) : (h + 1) * (E // HALVES)]
-            nc.scalar.dma_start(weights_half[:], experts.rearrange("e k m -> k e m"))
-            weights.append(weights_half)
+        rows = held.tile([P, BLOCKS, K], BF16, name="rows")
+        nc.scalar.dma_start(rows[:], table.rearrange("(b p) k -> p b k", p=P))
+        weights = held.tile([K, E, M], BF16, name="weights")
+        nc.scalar.dma_start(weights[:], w.rearrange("e k m -> k e m"))
 
         zeros = held.tile([P, P], BF16, name="zeros")
         nc.gpsimd.memset(zeros[:], 0.0)
@@ -73,8 +65,9 @@ def tile_gather_matmul_kernel(tc, table, w, c, offs, out):
         tokens = held.tile([K, S], BF16, name="tokens")
         for h in range(HALVES):
             flipped = psum.tile([K, S // HALVES], BF16, name=f"flipped{h}")
-            for b in range(BLOCKS // HALVES):
-                nc.tensor.transpose(flipped[:, b * P : (b + 1) * P], rows[h][:, b, :], identity[:])
+            for i in range(BLOCKS // HALVES):
+                b = h * (BLOCKS // HALVES) + i
+                nc.tensor.transpose(flipped[:, i * P : (i + 1) * P], rows[:, b, :], identity[:])
             nc.vector.tensor_copy(tokens[:, h * (S // HALVES) : (h + 1) * (S // HALVES)], flipped[:])
 
         scaled = held.tile([M, N], F32, name="scaled")
@@ -86,7 +79,7 @@ def tile_gather_matmul_kernel(tc, table, w, c, offs, out):
                 picked = tokens[:].indirect(offsets[:, e * LIST_COLUMNS : (e + 1) * LIST_COLUMNS])
                 nc.tensor.matmul(
                     product[:, i * Q : (i + 1) * Q],
-                    weights[e // (E // HALVES)][:, e % (E // HALVES), :],
+                    weights[:, e, :],
                     picked,
                     start=True,
                     stop=True,

@@ -35,11 +35,12 @@ def tile_gather_matmul_kernel(tc, table, w, c, offs, out):
         weights = held.tile([K, E, M], BF16, name="weights")
         nc.scalar.dma_start(weights[:], w.rearrange("e k m -> k e m"))
 
-        zeros = held.tile([P, P], BF16, name="zeros")
+        zeros = held.tile([P, 2], BF16, name="zeros")
         nc.gpsimd.memset(zeros[:], 0.0)
+        zero_matrix = zeros[:, 0:1].to_broadcast([P, P])
         unread = psum.tile([P, P], F32, name="unread")
         for i in range(WARM_UPS):
-            nc.tensor.matmul(unread[:], zeros[:], zeros[:], start=True, stop=True)
+            nc.tensor.matmul(unread[:], zero_matrix, zero_matrix, start=True, stop=True)
 
         identity = held.tile([P, P], BF16, name="identity")
         make_identity(nc, identity[:])

@@ -31,7 +31,10 @@ def tile_gather_matmul_kernel(tc, table, w, c, offs, out):
         offsets = held.tile([P, N // 16], U16, name="offsets")
         nc.sync.dma_start(offsets[:], offs)
         rows = held.tile([P, BLOCKS, K], BF16, name="rows")
-        nc.scalar.dma_start(rows[:], table.rearrange("(b p) k -> p b k", p=P))
+        blocks_first = table.rearrange("(b p) k -> p b k", p=P)
+        for h in range(HALVES):
+            half = slice(h * (BLOCKS // HALVES), (h + 1) * (BLOCKS // HALVES))
+            nc.scalar.dma_start(rows[:, half, :], blocks_first[:, half, :])
         weights = held.tile([K, E, M], BF16, name="weights")
         nc.scalar.dma_start(weights[:], w.rearrange("e k m -> k e m"))
 
@@ -88,5 +91,7 @@ def tile_gather_matmul_kernel(tc, table, w, c, offs, out):
             nc.vector.tensor_tensor(
                 scaled[:, columns], product[:], gains[:, columns], mybir.AluOpType.mult
             )
-            queue = nc.sync if g % 2 == 0 else nc.scalar
-            queue.dma_start(out[:, columns], scaled[:, columns])
+            if g > 0:
+                unstored = slice(0 if g == 1 else columns.start, columns.stop)
+                queue = nc.sync if g % 2 == 1 else nc.scalar
+                queue.dma_start(out[:, unstored], scaled[:, unstored])

@@ -31,12 +31,12 @@ def tile_gather_matmul_kernel(tc, table, w, c, offs, out):
         offsets = held.tile([P, N // 16], U16, name="offsets")
         nc.sync.dma_start(offsets[:], offs)
         rows = held.tile([P, BLOCKS, K], BF16, name="rows")
-        blocks_first = table.rearrange("(b p) k -> p b k", p=P)
-        for h in range(HALVES):
-            half = slice(h * (BLOCKS // HALVES), (h + 1) * (BLOCKS // HALVES))
-            nc.scalar.dma_start(rows[:, half, :], blocks_first[:, half, :])
+        nc.scalar.dma_start(rows[:], table.rearrange("(b p) k -> p b k", p=P))
         weights = held.tile([K, E, M], BF16, name="weights")
-        nc.scalar.dma_start(weights[:], w.rearrange("e k m -> k e m"))
+        contraction_first = w.rearrange("e k m -> k e m")
+        for h in range(HALVES):
+            half = slice(h * (E // HALVES), (h + 1) * (E // HALVES))
+            nc.scalar.dma_start(weights[:, half, :], contraction_first[:, half, :])
 
         zeros = held.tile([P, 2], BF16, name="zeros")
         nc.gpsimd.memset(zeros[:], 0.0)

import concourse.mybir as mybir
from concourse.masks import make_identity

BF16, F32, U16 = mybir.dt.bfloat16, mybir.dt.float32, mybir.dt.uint16

P = 128
S = 512
K = 128
M = 128
N = 512
E = 8
Q = N // E
LIST_COLUMNS = Q // 16
HALVES = 2
PIECES = 4
BLOCKS = S // P
STRIDE = N // P
WARM_UPS = 12

FLOPS = 2 * K * M * N


def tile_gather_matmul_kernel(tc, table, w, c, offs, out):
    nc = tc.nc
    with (
        tc.tile_pool(name="held", bufs=1) as held,
        tc.psum_pool(name="psum", bufs=1) as psum,
    ):
        gain_columns = held.tile([P, STRIDE], F32, name="gain_columns")
        nc.sync.dma_start(gain_columns[:], c.rearrange("o (p r) -> p (o r)", r=STRIDE))
        offsets = held.tile([P, N // 16], U16, name="offsets")
        nc.sync.dma_start(offsets[:], offs)
        rows = held.tile([P, BLOCKS, K], BF16, name="rows")
        nc.scalar.dma_start(rows[:], table.rearrange("(b p) k -> p b k", p=P))
        weights = held.tile([K, E, M], BF16, name="weights")
        contraction_first = w.rearrange("e k m -> k e m")
        for h in range(HALVES):
            half = slice(h * (E // HALVES), (h + 1) * (E // HALVES))
            nc.scalar.dma_start(weights[:, half, :], contraction_first[:, half, :])

        zeros = held.tile([P, 2], BF16, name="zeros")
        nc.gpsimd.memset(zeros[:], 0.0)
        zero_matrix = zeros[:, 0:1].to_broadcast([P, P])
        unread = psum.tile([P, P], F32, name="unread")
        for i in range(WARM_UPS):
            nc.tensor.matmul(unread[:], zero_matrix, zero_matrix, start=True, stop=True)

        identity = held.tile([P, P], BF16, name="identity")
        make_identity(nc, identity[:])
        identity32 = held.tile([P, P], F32, name="identity32")
        nc.vector.tensor_copy(identity32[:], identity[:])
        spread = psum.tile([M, N], F32, name="spread")
        for r in range(STRIDE):
            nc.tensor.transpose(
                spread[:, r * P : (r + 1) * P],
                gain_columns[:, r : r + 1].to_broadcast([P, M]),
                identity32[:],
            )
        in_list_order = spread[:].rearrange("m (r p) -> m p r", r=STRIDE)
        gains = held.tile([M, N], F32, name="gains")
        for h in range(HALVES):
            nc.scalar.copy(
                gains[:, h * (N // HALVES) : (h + 1) * (N // HALVES)].rearrange(
                    "m (p r) -> m p r", r=STRIDE
                ),
                in_list_order[:, h * (P // HALVES) : (h + 1) * (P // HALVES), :],
            )

        tokens = held.tile([K, S], BF16, name="tokens")
        for h in range(HALVES):
            flipped = psum.tile([K, S // HALVES], BF16, name=f"flipped{h}")
            for i in range(BLOCKS // HALVES):
                b = h * (BLOCKS // HALVES) + i
                nc.tensor.transpose(flipped[:, i * P : (i + 1) * P], rows[:, b, :], identity[:])
            nc.vector.tensor_copy(tokens[:, h * (S // HALVES) : (h + 1) * (S // HALVES)], flipped[:])

        scaled = held.tile([M, N], F32, name="scaled")
        for g in range(PIECES):
            columns = slice(g * (N // PIECES), (g + 1) * (N // PIECES))
            product = psum.tile([M, N // PIECES], F32, name=f"product{g}")
            for i in range(E // PIECES):
                e = g * (E // PIECES) + i
                picked = tokens[:].indirect(offsets[:, e * LIST_COLUMNS : (e + 1) * LIST_COLUMNS])
                nc.tensor.matmul(
                    product[:, i * Q : (i + 1) * Q],
                    weights[:, e, :],
                    picked,
                    start=True,
                    stop=True,
                )
            nc.vector.tensor_tensor(
                scaled[:, columns], product[:], gains[:, columns], mybir.AluOpType.mult
            )
            if g > 0:
                unstored = slice(0 if g == 1 else columns.start, columns.stop)
                queue = nc.sync if g % 2 == 1 else nc.scalar
                queue.dma_start(out[:, unstored], scaled[:, unstored])
